import numpy as np
import ml_dtypes


def mxq(x, axis, fmt="e4m3"):
    dtype, down = {"e4m3": (ml_dtypes.float8_e4m3fn, 7), "e5m2": (ml_dtypes.float8_e5m2, 14)}[fmt]
    v = np.moveaxis(np.asarray(x, np.float32).astype(ml_dtypes.bfloat16).astype(np.float64), axis, -1)
    blocks = v.reshape(v.shape[:-1] + (-1, 32))
    amax = np.abs(blocks).max(-1, keepdims=True)
    byte = np.maximum(np.where(amax > 0, np.frexp(amax)[1] - 1 + 127, 0) - down, 1)
    scale = np.exp2(byte - 127.0)
    codes = (blocks / scale).astype(np.float32).astype(dtype).astype(np.float64)
    return np.moveaxis((codes * scale).reshape(v.shape), -1, axis)


WIDE = False


def mx_kscale(k):
    if not WIDE:
        return np.ones(k)
    levels = np.array([18, -18])
    if k % 512:
        return np.exp2(np.random.permutation(np.resize(levels, k // 32))).repeat(32)
    a = np.empty((k // 512, 16))
    for p in range(k // 512):
        a[p, :8] = np.random.permutation(np.resize(levels, 8))
        for g in range(8):
            far = levels[np.abs(levels - a[p, g]) >= 10]
            a[p, g + 8] = far[np.random.randint(len(far))]
    return np.exp2(a.ravel()).repeat(32)


def f64(x):
    return np.asarray(x).astype(np.float64)


def striped(idx):
    return np.tile(np.asarray(idx).reshape(-1, 16).T, (8, 1)).astype(np.uint16)


def unstriped(offs):
    return offs[:16].T.reshape(-1).astype(np.int64)


B, N, T, D, DV, NQ = 1, 512, 1024, 128, 0, 1024


def setup_inputs():
    n = np.random.standard_normal
    idx = np.sort(np.random.permutation(T)[:B * N].reshape(B, N), axis=1).reshape(-1)
    z = mx_kscale(NQ)[:, None]
    return {
        "g": (n((B, NQ, N)) * z / np.sqrt(NQ)).astype(np.float32),
        "qm": (n((B, NQ, D)) / z).astype(np.float32),
        "offs": striped(idx),
    }


def reference(g, qm, offs):
    idx = unstriped(offs)
    dk = mxq(f64(qm), 1, "e4m3").transpose(0, 2, 1) @ mxq(f64(g), 1, "e5m2")
    out = np.zeros((D, T))
    out[:, idx] = dk.transpose(1, 0, 2).reshape(D, B * N)
    return out

@@ -1,0 +1,102 @@
+from contextlib import ExitStack
+
+import concourse.mybir as mybir
+
+Q, SLOTS, TOKENS, D = 1024, 512, 1024, 128
+
+FLOPS = 2 * Q * SLOTS * D
+
+F32 = mybir.dt.float32
+BF16 = mybir.dt.bfloat16
+U32 = mybir.dt.uint32
+U16 = mybir.dt.uint16
+U8 = mybir.dt.uint8
+E4M3X4 = mybir.dt.float8_e4m3fn_x4
+E5M2X4 = mybir.dt.float8_e5m2_x4
+
+P = 128
+PACK = 4
+PASSES = Q // (P * PACK)
+
+
+def tile_attend_dk_kernel(tc, g, qm, offs, out):
+    nc = tc.nc
+    g_rows = g.rearrange("b (c p j) n -> (b c) p j n", p=P, j=PACK)
+    qm_rows = qm.rearrange("b (c p j) d -> (b c) p j d", p=P, j=PACK)
+
+    with ExitStack() as ctx:
+        held = ctx.enter_context(tc.tile_pool(name="held", bufs=1))
+        psum = ctx.enter_context(tc.psum_pool(name="psum", bufs=1))
+
+        offsets = held.tile([P, SLOTS // 16], U16, name="offsets")
+        placed = held.tile([P, TOKENS], F32, name="placed")
+        sums = held.tile([P, SLOTS], F32, name="sums")
+        acc = psum.tile([D, SLOTS], F32, name="acc")
+
+        def load(rows, width, name):
+            raw = held.tile([P, PACK, width], F32, name=name)
+            nc.sync.dma_start(out=raw[:], in_=rows)
+            return raw
+
+        g0 = load(g_rows[0], SLOTS, "g0")
+        qm0 = load(qm_rows[0], D, "qm0")
+        g1a = load(g_rows[1][:, :, 0:256], 256, "g1a")
+        g1b = load(g_rows[1][:, :, 256:512], 256, "g1b")
+        qm1 = load(qm_rows[1], D, "qm1")
+        nc.sync.dma_start(offsets[:], offs)
+
+        nc.vector.memset(placed[:], 0.0)
+
+        g_codes = [held.tile([P, SLOTS], U32, name=f"g_codes{c}", align_bytes=64) for c in range(PASSES)]
+        g_scales = [held.tile([P, SLOTS], U8, name=f"g_scales{c}", align_bytes=64) for c in range(PASSES)]
+        q_codes = [held.tile([P, D], U32, name=f"q_codes{c}", align_bytes=64) for c in range(PASSES)]
+        q_scales = [held.tile([P, D], U8, name=f"q_scales{c}", align_bytes=64) for c in range(PASSES)]
+
+        def cast(copy, raw, lo, hi, name):
+            grouped = held.tile([P, hi - lo, PACK], BF16, name=name, align_bytes=64)
+            copy(grouped[:], raw[:, :, lo:hi].rearrange("p j w -> p w j"))
+            return grouped
+
+        def quantize(grouped, codes, scales, lo, hi, dtype):
+            nc.vector.quantize_mx(
+                out=codes[:, lo:hi].bitcast(dtype),
+                scales=scales[:, lo:hi],
+                in_=grouped[:].rearrange("p w j -> p (w j)"),
+            )
+
+        def multiply(c):
+            nc.tensor.matmul_mx(
+                out=acc[:],
+                lhsT=q_codes[c][:].bitcast(E4M3X4),
+                lhsT_scale=q_scales[c][:],
+                rhs=g_codes[c][:].bitcast(E5M2X4),
+                rhs_scale=g_scales[c][:],
+                start=(c == 0),
+                stop=(c == PASSES - 1),
+            )
+
+        v, s = nc.vector.tensor_copy, nc.scalar.copy
+        b_g0v = cast(v, g0, 0, 256, "b_g0v")
+        b_g0s = cast(s, g0, 256, 512, "b_g0s")
+        b_q0 = cast(v, qm0, 0, D, "b_q0")
+        quantize(b_g0v, g_codes[0], g_scales[0], 0, 256, E5M2X4)
+        quantize(b_q0, q_codes[0], q_scales[0], 0, D, E4M3X4)
+        quantize(b_g0s, g_codes[0], g_scales[0], 256, 512, E5M2X4)
+        multiply(0)
+
+        b_av = cast(v, g1a, 0, 128, "b_av")
+        b_as = cast(s, g1a, 128, 256, "b_as")
+        b_bv = cast(v, g1b, 0, 128, "b_bv")
+        b_bs = cast(s, g1b, 128, 256, "b_bs")
+        quantize(b_av, g_codes[1], g_scales[1], 0, 128, E5M2X4)
+        quantize(b_as, g_codes[1], g_scales[1], 128, 256, E5M2X4)
+        b_q1 = cast(v, qm1, 0, D, "b_q1")
+        quantize(b_bv, g_codes[1], g_scales[1], 256, 384, E5M2X4)
+        quantize(b_bs, g_codes[1], g_scales[1], 384, 512, E5M2X4)
+        quantize(b_q1, q_codes[1], q_scales[1], 0, D, E4M3X4)
+        multiply(1)
+
+        for lo, hi in ((0, 128), (128, 512)):
+            nc.scalar.copy(sums[:, lo:hi], acc[:, lo:hi])
+            nc.vector.tensor_copy(placed[:].indirect(offsets[:, lo // 16 : hi // 16]), sums[:, lo:hi])
+        nc.sync.dma_start(out=out, in_=placed[:])

@@ -38,11 +38,13 @@ def tile_attend_dk_kernel(tc, g, qm, offs, out):
             nc.sync.dma_start(out=raw[:], in_=rows)
             return raw
 
-        g0 = load(g_rows[0], SLOTS, "g0")
-        qm0 = load(qm_rows[0], D, "qm0")
-        g1a = load(g_rows[1][:, :, 0:256], 256, "g1a")
-        g1b = load(g_rows[1][:, :, 256:512], 256, "g1b")
-        qm1 = load(qm_rows[1], D, "qm1")
+        def load_pair(c, h):
+            raw = held.tile([P, 2, SLOTS], F32, name=f"g_raw{c}{h}")
+            nc.sync.dma_start(out=raw[:], in_=g_rows[c][:, 2 * h : 2 * h + 2, :])
+            return raw
+
+        g_raw = [[load_pair(c, h) for h in range(2)] for c in range(PASSES)]
+        q_raw = [load(qm_rows[c], D, f"q_raw{c}") for c in range(PASSES)]
         nc.sync.dma_start(offsets[:], offs)
 
         nc.vector.memset(placed[:], 0.0)
@@ -52,16 +54,11 @@ def tile_attend_dk_kernel(tc, g, qm, offs, out):
         q_codes = [held.tile([P, D], U32, name=f"q_codes{c}", align_bytes=64) for c in range(PASSES)]
         q_scales = [held.tile([P, D], U8, name=f"q_scales{c}", align_bytes=64) for c in range(PASSES)]
 
-        def cast(copy, raw, lo, hi, name):
-            grouped = held.tile([P, hi - lo, PACK], BF16, name=name, align_bytes=64)
-            copy(grouped[:], raw[:, :, lo:hi].rearrange("p j w -> p w j"))
-            return grouped
-
         def quantize(grouped, codes, scales, lo, hi, dtype):
             nc.vector.quantize_mx(
                 out=codes[:, lo:hi].bitcast(dtype),
                 scales=scales[:, lo:hi],
-                in_=grouped[:].rearrange("p w j -> p (w j)"),
+                in_=grouped[:, lo:hi, :].rearrange("p w j -> p (w j)"),
             )
 
         def multiply(c):
@@ -76,24 +73,27 @@ def tile_attend_dk_kernel(tc, g, qm, offs, out):
             )
 
         v, s = nc.vector.tensor_copy, nc.scalar.copy
-        b_g0v = cast(v, g0, 0, 256, "b_g0v")
-        b_g0s = cast(s, g0, 256, 512, "b_g0s")
-        b_q0 = cast(v, qm0, 0, D, "b_q0")
-        quantize(b_g0v, g_codes[0], g_scales[0], 0, 256, E5M2X4)
-        quantize(b_q0, q_codes[0], q_scales[0], 0, D, E4M3X4)
-        quantize(b_g0s, g_codes[0], g_scales[0], 256, 512, E5M2X4)
-        multiply(0)
+        HALF = SLOTS // 2
+        gb = [held.tile([P, SLOTS, PACK], BF16, name=f"gb{c}", align_bytes=64) for c in range(PASSES)]
+        qb = [held.tile([P, D, PACK], BF16, name=f"qb{c}", align_bytes=64) for c in range(PASSES)]
 
-        b_av = cast(v, g1a, 0, 128, "b_av")
-        b_as = cast(s, g1a, 128, 256, "b_as")
-        b_bv = cast(v, g1b, 0, 128, "b_bv")
-        b_bs = cast(s, g1b, 128, 256, "b_bs")
-        quantize(b_av, g_codes[1], g_scales[1], 0, 128, E5M2X4)
-        quantize(b_as, g_codes[1], g_scales[1], 128, 256, E5M2X4)
-        b_q1 = cast(v, qm1, 0, D, "b_q1")
-        quantize(b_bv, g_codes[1], g_scales[1], 256, 384, E5M2X4)
-        quantize(b_bs, g_codes[1], g_scales[1], 384, 512, E5M2X4)
-        quantize(b_q1, q_codes[1], q_scales[1], 0, D, E4M3X4)
+        def cast_pair(c, h, cut):
+            planes = slice(2 * h, 2 * h + 2)
+            v(gb[c][:, :cut, planes], g_raw[c][h][:, :, :cut].rearrange("p j w -> p w j"))
+            s(gb[c][:, cut:, planes], g_raw[c][h][:, :, cut:].rearrange("p j w -> p w j"))
+
+        cast_pair(0, 0, 192)
+        cast_pair(0, 1, 192)
+        quantize(gb[0], g_codes[0], g_scales[0], 0, SLOTS, E5M2X4)
+        cast_pair(1, 0, 192)
+        cast_pair(1, 1, 320)
+        quantize(gb[1], g_codes[1], g_scales[1], 0, HALF, E5M2X4)
+        v(qb[0][:], q_raw[0][:].rearrange("p j w -> p w j"))
+        quantize(qb[0], q_codes[0], q_scales[0], 0, D, E4M3X4)
+        multiply(0)
+        quantize(gb[1], g_codes[1], g_scales[1], HALF, SLOTS, E5M2X4)
+        v(qb[1][:], q_raw[1][:].rearrange("p j w -> p w j"))
+        quantize(qb[1], q_codes[1], q_scales[1], 0, D, E4M3X4)
         multiply(1)
 
         for lo, hi in ((0, 128), (128, 512)):

@@ -43,8 +43,9 @@ def tile_attend_dk_kernel(tc, g, qm, offs, out):
             nc.sync.dma_start(out=raw[:], in_=g_rows[c][:, 2 * h : 2 * h + 2, :])
             return raw
 
+        q_raw0 = load(qm_rows[0], D, "q_raw0")
         g_raw = [[load_pair(c, h) for h in range(2)] for c in range(PASSES)]
-        q_raw = [load(qm_rows[c], D, f"q_raw{c}") for c in range(PASSES)]
+        q_raw1 = load(qm_rows[1], D, "q_raw1")
         nc.sync.dma_start(offsets[:], offs)
 
         nc.vector.memset(placed[:], 0.0)
@@ -82,18 +83,25 @@ def tile_attend_dk_kernel(tc, g, qm, offs, out):
             v(gb[c][:, :cut, planes], g_raw[c][h][:, :, :cut].rearrange("p j w -> p w j"))
             s(gb[c][:, cut:, planes], g_raw[c][h][:, :, cut:].rearrange("p j w -> p w j"))
 
-        cast_pair(0, 0, 192)
-        cast_pair(0, 1, 192)
-        quantize(gb[0], g_codes[0], g_scales[0], 0, SLOTS, E5M2X4)
-        cast_pair(1, 0, 192)
-        cast_pair(1, 1, 320)
-        quantize(gb[1], g_codes[1], g_scales[1], 0, HALF, E5M2X4)
-        v(qb[0][:], q_raw[0][:].rearrange("p j w -> p w j"))
+        def cast_q(c, raw):
+            v(
+                qb[c][:].rearrange("p (b i) j -> p b j i", i=4),
+                raw[:].rearrange("p j (b i) -> p b j i", i=4),
+            )
+
+        cast_q(0, q_raw0)
         quantize(qb[0], q_codes[0], q_scales[0], 0, D, E4M3X4)
+        cast_pair(0, 0, HALF)
+        cast_pair(0, 1, HALF)
+        quantize(gb[0], g_codes[0], g_scales[0], 0, HALF, E5M2X4)
+        quantize(gb[0], g_codes[0], g_scales[0], HALF, SLOTS, E5M2X4)
         multiply(0)
-        quantize(gb[1], g_codes[1], g_scales[1], HALF, SLOTS, E5M2X4)
-        v(qb[1][:], q_raw[1][:].rearrange("p j w -> p w j"))
+        cast_pair(1, 0, HALF)
+        cast_pair(1, 1, HALF)
+        cast_q(1, q_raw1)
+        quantize(gb[1], g_codes[1], g_scales[1], 0, HALF, E5M2X4)
         quantize(qb[1], q_codes[1], q_scales[1], 0, D, E4M3X4)
+        quantize(gb[1], g_codes[1], g_scales[1], HALF, SLOTS, E5M2X4)
         multiply(1)
 
         for lo, hi in ((0, 128), (128, 512)):

@@ -83,13 +83,13 @@ def tile_attend_dk_kernel(tc, g, qm, offs, out):
             v(gb[c][:, :cut, planes], g_raw[c][h][:, :, :cut].rearrange("p j w -> p w j"))
             s(gb[c][:, cut:, planes], g_raw[c][h][:, :, cut:].rearrange("p j w -> p w j"))
 
-        def cast_q(c, raw):
-            v(
+        def cast_q(c, raw, copy):
+            copy(
                 qb[c][:].rearrange("p (b i) j -> p b j i", i=4),
                 raw[:].rearrange("p j (b i) -> p b j i", i=4),
             )
 
-        cast_q(0, q_raw0)
+        cast_q(0, q_raw0, v)
         quantize(qb[0], q_codes[0], q_scales[0], 0, D, E4M3X4)
         cast_pair(0, 0, HALF)
         cast_pair(0, 1, HALF)
@@ -97,14 +97,14 @@ def tile_attend_dk_kernel(tc, g, qm, offs, out):
         quantize(gb[0], g_codes[0], g_scales[0], HALF, SLOTS, E5M2X4)
         multiply(0)
         cast_pair(1, 0, HALF)
-        cast_pair(1, 1, HALF)
-        cast_q(1, q_raw1)
+        cast_pair(1, 1, 320)
+        cast_q(1, q_raw1, s)
         quantize(gb[1], g_codes[1], g_scales[1], 0, HALF, E5M2X4)
         quantize(qb[1], q_codes[1], q_scales[1], 0, D, E4M3X4)
         quantize(gb[1], g_codes[1], g_scales[1], HALF, SLOTS, E5M2X4)
         multiply(1)
 
-        for lo, hi in ((0, 128), (128, 512)):
+        for lo, hi in ((0, 512),):
             nc.scalar.copy(sums[:, lo:hi], acc[:, lo:hi])
             nc.vector.tensor_copy(placed[:].indirect(offsets[:, lo // 16 : hi // 16]), sums[:, lo:hi])
         nc.sync.dma_start(out=out, in_=placed[:])

from contextlib import ExitStack

import concourse.mybir as mybir

Q, SLOTS, TOKENS, D = 1024, 512, 1024, 128

FLOPS = 2 * Q * SLOTS * D

F32 = mybir.dt.float32
BF16 = mybir.dt.bfloat16
U32 = mybir.dt.uint32
U16 = mybir.dt.uint16
U8 = mybir.dt.uint8
E4M3X4 = mybir.dt.float8_e4m3fn_x4
E5M2X4 = mybir.dt.float8_e5m2_x4

P = 128
PACK = 4
PASSES = Q // (P * PACK)


def tile_attend_dk_kernel(tc, g, qm, offs, out):
    nc = tc.nc
    g_rows = g.rearrange("b (c p j) n -> (b c) p j n", p=P, j=PACK)
    qm_rows = qm.rearrange("b (c p j) d -> (b c) p j d", p=P, j=PACK)

    with ExitStack() as ctx:
        held = ctx.enter_context(tc.tile_pool(name="held", bufs=1))
        psum = ctx.enter_context(tc.psum_pool(name="psum", bufs=1))

        offsets = held.tile([P, SLOTS // 16], U16, name="offsets")
        placed = held.tile([P, TOKENS], F32, name="placed")
        sums = held.tile([P, SLOTS], F32, name="sums")
        acc = psum.tile([D, SLOTS], F32, name="acc")

        def load(rows, width, name):
            raw = held.tile([P, PACK, width], F32, name=name)
            nc.sync.dma_start(out=raw[:], in_=rows)
            return raw

        def load_pair(c, h):
            raw = held.tile([P, 2, SLOTS], F32, name=f"g_raw{c}{h}")
            nc.sync.dma_start(out=raw[:], in_=g_rows[c][:, 2 * h : 2 * h + 2, :])
            return raw

        q_raw0 = load(qm_rows[0], D, "q_raw0")
        g_raw = [[load_pair(c, h) for h in range(2)] for c in range(PASSES)]
        q_raw1 = load(qm_rows[1], D, "q_raw1")
        nc.sync.dma_start(offsets[:], offs)

        nc.vector.memset(placed[:], 0.0)

        g_codes = [held.tile([P, SLOTS], U32, name=f"g_codes{c}", align_bytes=64) for c in range(PASSES)]
        g_scales = [held.tile([P, SLOTS], U8, name=f"g_scales{c}", align_bytes=64) for c in range(PASSES)]
        q_codes = [held.tile([P, D], U32, name=f"q_codes{c}", align_bytes=64) for c in range(PASSES)]
        q_scales = [held.tile([P, D], U8, name=f"q_scales{c}", align_bytes=64) for c in range(PASSES)]

        def quantize(grouped, codes, scales, lo, hi, dtype):
            nc.vector.quantize_mx(
                out=codes[:, lo:hi].bitcast(dtype),
                scales=scales[:, lo:hi],
                in_=grouped[:, lo:hi, :].rearrange("p w j -> p (w j)"),
            )

        def multiply(c):
            nc.tensor.matmul_mx(
                out=acc[:],
                lhsT=q_codes[c][:].bitcast(E4M3X4),
                lhsT_scale=q_scales[c][:],
                rhs=g_codes[c][:].bitcast(E5M2X4),
                rhs_scale=g_scales[c][:],
                start=(c == 0),
                stop=(c == PASSES - 1),
            )

        v, s = nc.vector.tensor_copy, nc.scalar.copy
        HALF = SLOTS // 2
        gb = [held.tile([P, SLOTS, PACK], BF16, name=f"gb{c}", align_bytes=64) for c in range(PASSES)]
        qb = [held.tile([P, D, PACK], BF16, name=f"qb{c}", align_bytes=64) for c in range(PASSES)]

        def cast_pair(c, h, cut):
            planes = slice(2 * h, 2 * h + 2)
            v(gb[c][:, :cut, planes], g_raw[c][h][:, :, :cut].rearrange("p j w -> p w j"))
            s(gb[c][:, cut:, planes], g_raw[c][h][:, :, cut:].rearrange("p j w -> p w j"))

        def cast_q(c, raw, copy):
            copy(
                qb[c][:].rearrange("p (b i) j -> p b j i", i=4),
                raw[:].rearrange("p j (b i) -> p b j i", i=4),
            )

        cast_q(0, q_raw0, v)
        quantize(qb[0], q_codes[0], q_scales[0], 0, D, E4M3X4)
        cast_pair(0, 0, HALF)
        cast_pair(0, 1, HALF)
        quantize(gb[0], g_codes[0], g_scales[0], 0, HALF, E5M2X4)
        quantize(gb[0], g_codes[0], g_scales[0], HALF, SLOTS, E5M2X4)
        multiply(0)
        cast_pair(1, 0, HALF)
        cast_pair(1, 1, 320)
        cast_q(1, q_raw1, s)
        quantize(gb[1], g_codes[1], g_scales[1], 0, HALF, E5M2X4)
        quantize(qb[1], q_codes[1], q_scales[1], 0, D, E4M3X4)
        quantize(gb[1], g_codes[1], g_scales[1], HALF, SLOTS, E5M2X4)
        multiply(1)

        for lo, hi in ((0, 512),):
            nc.scalar.copy(sums[:, lo:hi], acc[:, lo:hi])
            nc.vector.tensor_copy(placed[:].indirect(offsets[:, lo // 16 : hi // 16]), sums[:, lo:hi])
        nc.sync.dma_start(out=out, in_=placed[:])
